import numpy as np
import ml_dtypes


def mxq(x, axis, fmt="e4m3"):
    dtype, down = {"e4m3": (ml_dtypes.float8_e4m3fn, 7), "e5m2": (ml_dtypes.float8_e5m2, 14)}[fmt]
    v = np.moveaxis(np.asarray(x, np.float32).astype(ml_dtypes.bfloat16).astype(np.float64), axis, -1)
    blocks = v.reshape(v.shape[:-1] + (-1, 32))
    amax = np.abs(blocks).max(-1, keepdims=True)
    byte = np.maximum(np.where(amax > 0, np.frexp(amax)[1] - 1 + 127, 0) - down, 1)
    scale = np.exp2(byte - 127.0)
    codes = (blocks / scale).astype(np.float32).astype(dtype).astype(np.float64)
    return np.moveaxis((codes * scale).reshape(v.shape), -1, axis)


WIDE = False


def mx_kscale(k):
    if not WIDE:
        return np.ones(k)
    levels = np.array([10, -10, 5, -5, 0])
    if k % 512:
        return np.exp2(np.random.permutation(np.resize(levels, k // 32))).repeat(32)
    a = np.empty((k // 512, 16))
    for p in range(k // 512):
        a[p, :8] = np.random.permutation(np.resize(levels, 8))
        for g in range(8):
            far = levels[np.abs(levels - a[p, g]) >= 10]
            a[p, g + 8] = far[np.random.randint(len(far))]
    return np.exp2(a.ravel()).repeat(32)


def f64(x):
    return np.asarray(x).astype(np.float64)


def striped(idx):
    return np.tile(idx.reshape(-1, 16).T, (8, 1)).astype(np.uint16)


def unstriped(offs):
    return offs[:16].T.reshape(-1).astype(np.int64)


def striped8(idx):
    return np.concatenate([x.reshape(-1, 16).T for x in idx]).astype(np.uint16)


def runs(offs, k):
    lists = np.stack([offs[16 * r : 16 * r + 16].T.reshape(-1) for r in range(8)]).astype(np.int64)
    return lists[np.arange(k) % 512 // 64]


def pack_weight(w):
    k, n = w.shape
    w = f64(np.asarray(w, np.float32).astype(ml_dtypes.bfloat16)).reshape(k // 32, 32, n)
    amax = np.abs(w).max(1)
    byte = np.clip(np.where(amax > 0, np.frexp(amax)[1] - 1 + 127 - 7, 1), 1, 254)
    scaled = (w * np.exp2(127.0 - byte)[:, None, :]).reshape(k, n).astype(np.float32)
    words = np.ascontiguousarray(scaled.reshape(k // 512, 128, 4, n).transpose(0, 1, 3, 2)).astype(ml_dtypes.float8_e4m3fn).view(np.uint8)
    return words, np.ascontiguousarray(byte.astype(np.uint8).reshape(k // 512, 16, n))


def unpack_weight(words, scales):
    g, p, n, _ = words.shape
    vals = np.ascontiguousarray(words).view(ml_dtypes.float8_e4m3fn).astype(np.float64) * np.repeat(np.exp2(scales.astype(np.float64) - 127.0), 8, axis=1)[..., None]
    return vals.transpose(0, 1, 3, 2).reshape(g * 512, n)


def sigmoid(v):
    return 1.0 / (1.0 + np.exp(-np.maximum(v, -700.0)))

def planes(y):
    n, m = y.shape
    v = y.astype(np.float32).astype(ml_dtypes.bfloat16).astype(np.float64).reshape(n // 32, 32, m)
    top = np.abs(v).max(1)
    byte = np.clip(np.where(top > 0, np.frexp(top)[1] - 1 + 127 - 7, 1), 1, 254)
    codes = (v * np.exp2(127.0 - byte)[:, None, :]).reshape(n, m).astype(np.float32).astype(ml_dtypes.float8_e4m3fn).view(np.uint8)
    words = codes.reshape(n // 512, 128, 4, m).transpose(0, 1, 3, 2)
    return np.ascontiguousarray(words), np.ascontiguousarray(byte.astype(np.uint8).reshape(n // 512, 16, m))


K, T, S, H, G = 512, 1024, 512, 512, 2048


def setup_inputs():
    n = np.random.standard_normal
    s = mx_kscale(K)[:, None]
    packed_xT = pack_weight(n((K, T)) * s)
    packed_w1 = pack_weight(n((K, H)) / np.sqrt(K) / s)
    packed_w2 = pack_weight(n((K, H)) / np.sqrt(K) / s)
    packed_dT = pack_weight(n((K, G)) / s)
    return {
        "x_words": packed_xT[0],
        "x_scales": packed_xT[1],
        "w1_words": packed_w1[0],
        "w1_scales": packed_w1[1],
        "w2_words": packed_w2[0],
        "w2_scales": packed_w2[1],
        "gs": (np.random.uniform(0.5, 1.5, (K, 1)) * s).astype(np.float32),
        "d_words": packed_dT[0],
        "d_scales": packed_dT[1],
        "offs": striped(np.random.permutation(T)[:S]),
        "two": striped(np.random.permutation(T)[:S]),
        "n1": striped8(np.stack([np.random.permutation(S) for _ in range(8)])),
        "n2": striped8(np.stack([np.random.permutation(S) for _ in range(8)])),
        "k1": striped8(np.random.randint(0, G, (8, H))),
        "n3": striped8(np.stack([np.random.permutation(S) for _ in range(8)])),
        "n4": striped8(np.stack([np.random.permutation(S) for _ in range(8)])),
    }


def reference(x_words, x_scales, w1_words, w1_scales, w2_words, w2_scales, gs, d_words, d_scales, offs, two, n1, n2, k1, n3, n4):
    d_k1 = unpack_weight(d_words, d_scales)[np.arange(K)[:, None], runs(k1, K)]
    xq = unpack_weight(x_words, x_scales)[:, unstriped(offs)]
    y = unpack_weight(w1_words, w1_scales).T @ xq
    x_two = unpack_weight(x_words, x_scales)[:, unstriped(two)]
    d = unpack_weight(w2_words, w2_scales).T @ x_two
    z = f64(gs) * (y + (sigmoid(d[np.arange(H)[:, None], runs(n2, H)] - d)) * (y[np.arange(H)[:, None], runs(n1, H)] - y))
    h = 0.0625 * ((d_k1.T @ mxq(z, 0, "e4m3")))
    out_0 = (h * (h[np.arange(H)[:, None], runs(n3, H)])) * (np.tanh(h[np.arange(H)[:, None], runs(n4, H)]))
    return (out_0,) + planes(out_0)

@@ -1,0 +1,195 @@
+from contextlib import ExitStack
+
+import concourse.mybir as mybir
+
+K, T, S, H, G = 512, 1024, 512, 512, 2048
+FLOPS = 3 * 2 * 512 * 512 * 512
+
+F32 = mybir.dt.float32
+BF16 = mybir.dt.bfloat16
+I32 = mybir.dt.int32
+U32 = mybir.dt.uint32
+U16 = mybir.dt.uint16
+U8 = mybir.dt.uint8
+FP8X4 = mybir.dt.float8_e4m3fn_x4
+ALU = mybir.AluOpType
+ACT = mybir.ActivationFunctionType
+
+P = 128
+PACK = 4
+Z_CHUNKS = ((0, 256), (256, 384), (384, 512))
+O_CHUNKS = ((0, 256), (256, 384), (384, 512))
+
+
+def tile_picked_twqpullbcube_none_po_kernel(
+    tc, x_words, x_scales, w1_words, w1_scales, w2_words, w2_scales, gs, d_words, d_scales,
+    offs, two, n1, n2, k1, n3, n4, out_0, out_1, out_2,
+):
+    nc = tc.nc
+
+    def words_of(ap):
+        return ap[0].rearrange("p n t -> p (n t)").bitcast(I32)
+
+    with ExitStack() as ctx:
+        keep = ctx.enter_context(tc.tile_pool(name="keep", bufs=1))
+        psum = ctx.enter_context(tc.psum_pool(name="psum", bufs=1))
+
+        def new(name, shape, dtype):
+            return keep.tile(shape, dtype, name=name, align_bytes=64)
+
+        lists = {}
+
+        def load_list(name, ap):
+            lists[name] = new("list_" + name, [P, S // 16], U16)
+            nc.sync.dma_start(lists[name][:], ap)
+
+        xs = new("xs", [P, T], U8)
+        ws = new("ws", [P, H], U8)
+        ds = new("ds", [P, G], U8)
+        dsm = new("dsm", [P, H], U8)
+        xw = new("xw", [P, T], I32)
+        w1w = new("w1w", [P, H], I32)
+        w2w = new("w2w", [P, H], I32)
+        dw = new("dw", [P, G], I32)
+        gain = new("gain", [P, PACK], F32)
+        warm = new("warm", [P, 8], F32)
+
+        nc.vector.memset(xs[:].bitcast(I32), 0)
+        nc.gpsimd.memset(ws[:].bitcast(I32), 0)
+        nc.gpsimd.memset(warm[:], 0.0)
+        nc.scalar.activation(warm[:, 0:1], warm[:, 1:2], ACT.Sigmoid)
+        nc.vector.memset(ds[:].bitcast(I32), 0)
+        nc.vector.memset(dsm[:].bitcast(I32), 0)
+        dwin = [new("dwin%d" % t, [P, 2 * S], F32) for t in range(PACK)]
+        dlast = new("dlast", [P, S], F32)
+        dcopy = [dwin[t + 1][:, S : 2 * S] for t in range(PACK - 1)] + [dlast[:]]
+        nc.vector.memset(dwin[0][:, S : 2 * S], 0.0)
+
+        load_list("two", two)
+        nc.sync.dma_start(xw[:], words_of(x_words))
+        load_list("offs", offs)
+        nc.sync.dma_start(w2w[:], words_of(w2_words))
+        for q in range(4):
+            nc.sync.dma_start(xs[32 * q : 32 * q + 4, :].bitcast(I32), x_scales[0, 4 * q : 4 * q + 4, :].bitcast(I32))
+        for q in range(4):
+            nc.sync.dma_start(ws[32 * q : 32 * q + 4, :].bitcast(I32), w2_scales[0, 4 * q : 4 * q + 4, :].bitcast(I32))
+        for q in range(4):
+            nc.sync.dma_start(ws[32 * q + 4 : 32 * q + 8, :].bitcast(I32), w1_scales[0, 4 * q : 4 * q + 4, :].bitcast(I32))
+        nc.sync.dma_start(w1w[:], words_of(w1_words))
+        load_list("n2", n2)
+        load_list("k1", k1)
+        nc.sync.dma_start(dw[:], words_of(d_words))
+        nc.sync.dma_start(gain[:], gs.rearrange("(p t) o -> p (t o)", t=PACK))
+        for e in range(2):
+            nc.sync.dma_start(ds[e:P:16, :].bitcast(I32), d_scales[0, e:16:2, :].bitcast(I32))
+        load_list("n1", n1)
+        load_list("n4", n4)
+        load_list("n3", n3)
+
+        def deal(name, src, dtype):
+            dealt = new(name, [P, H], dtype)
+            view = U32 if dtype == I32 else U8
+            nc.vector.tensor_copy(
+                dealt[:].bitcast(view).rearrange("p (t m) -> p m t", t=PACK),
+                src[:].bitcast(view).rearrange("p (m t) -> p m t", t=PACK),
+            )
+            return dealt
+
+        def pick(name, table, dtype, offsets):
+            picked = new(name, [P, S], dtype)
+            view = U32 if dtype == I32 else U8
+            nc.vector.tensor_copy(picked[:].bitcast(view), table[:].bitcast(view).indirect(offsets[:]))
+            return picked
+
+        banks_a = [psum.tile([P, S], F32, name="bank_a%d" % t, tag="bank_a%d" % t) for t in range(PACK)]
+        banks_b = [psum.tile([P, S], F32, name="bank_b%d" % t, tag="bank_b%d" % t) for t in range(PACK)]
+
+        def product(bank, words, scales, t, mov_words, mov_scales, lo, hi):
+            nc.tensor.matmul_mx(
+                out=bank[:, lo:hi],
+                lhsT=words[:, P * t : P * (t + 1)].bitcast(FP8X4),
+                lhsT_scale=scales[:, P * t : P * (t + 1)],
+                rhs=mov_words[:, lo:hi].bitcast(FP8X4),
+                rhs_scale=mov_scales[:, lo:hi],
+                start=True,
+                stop=True,
+            )
+
+        xw2 = pick("xw2", xw, I32, lists["two"])
+        xs2 = pick("xs2", xs, U8, lists["two"])
+        w2d = deal("w2d", w2w, I32)
+        wsd = deal("wsd", ws, U8)
+        for t in range(PACK):
+            product(banks_a[t], w2d, wsd[0:P], t, xw2, xs2, 0, S)
+            nc.scalar.copy(dwin[t][:, 0:S], banks_a[t][:])
+            nc.scalar.copy(dcopy[t], banks_a[t][:])
+        xw1 = pick("xw1", xw, I32, lists["offs"])
+        xs1 = pick("xs1", xs, U8, lists["offs"])
+        w1d = deal("w1d", w1w, I32)
+        ywin = [new("ywin%d" % t, [P, 2 * S], F32) for t in range(PACK)]
+        for t in range(PACK):
+            product(banks_b[t], w1d, wsd[4:P], t, xw1, xs1, 0, S)
+            nc.scalar.activation(ywin[t][:, 0:S], banks_b[t][:], ACT.Copy, scale=gain[:, t : t + 1])
+        gate = new("gate", [P, PACK, S], F32)
+        for t in range(PACK):
+            nc.vector.tensor_tensor(ywin[t][:, S : 2 * S], dwin[t][:].indirect(lists["n2"][:]), dcopy[t], ALU.subtract)
+            nc.scalar.activation(gate[:, t, :], ywin[t][:, S : 2 * S], ACT.Sigmoid)
+        dsg = pick("dsg", ds, U8, lists["k1"])
+        dsd = deal("dsd", dsg, U8)
+        for r, src in enumerate((0, 1, 16, 17)):
+            nc.sync.dma_start(dsm[r:P:32, :].bitcast(I32), dsd[src:P:32, :].bitcast(I32))
+        dwg = pick("dwg", dw, I32, lists["k1"])
+        dwd = deal("dwd", dwg, I32)
+
+        rest = new("rest", [P, PACK, S], F32)
+        for t in range(PACK):
+            nc.vector.scalar_tensor_tensor(rest[:, t, :], gate[:, t, :], 1.0, ywin[t][:, 0:S], ALU.subtract, ALU.mult)
+        pulled = new("pulled", [P, PACK, S], F32)
+        zw = new("zw", [P, S], I32)
+        zs = new("zs", [P, S], U8)
+        banks_h = [psum.tile([P, S], F32, name="bank_h%d" % t, tag="bank_a%d" % t) for t in range(PACK)]
+        hwin = [new("hwin%d" % t, [P, S], F32) for t in range(PACK)]
+        for lo, hi in Z_CHUNKS:
+            for t in range(PACK):
+                nc.vector.tensor_tensor(
+                    pulled[:, t, lo:hi], ywin[t][:].indirect(lists["n1"][:, lo // 16 : hi // 16]), gate[:, t, lo:hi], ALU.mult
+                )
+            zb = new("zb%d" % lo, [P, hi - lo, PACK], BF16)
+            nc.vector.tensor_tensor(
+                zb[:].rearrange("p (c i) t -> p c t i", i=4),
+                pulled[:, :, lo:hi].rearrange("p t (c i) -> p c t i", i=4),
+                rest[:, :, lo:hi].rearrange("p t (c i) -> p c t i", i=4),
+                ALU.subtract,
+            )
+            nc.vector.quantize_mx(out=zw[:, lo:hi].bitcast(FP8X4), scales=zs[:, lo:hi], in_=zb[:].rearrange("p j t -> p (j t)"))
+            for t in range(PACK):
+                product(banks_h[t], dwd, dsm[0:P], t, zw, zs, lo, hi)
+                nc.scalar.activation(dwin[t][:, lo:hi], banks_h[t][:, lo:hi], ACT.Tanh, scale=0.0625)
+                nc.scalar.activation(hwin[t][:, lo:hi], banks_h[t][:, lo:hi], ACT.Copy, scale=0.0625)
+
+        part = new("part", [P, PACK, S], F32)
+        for t in range(PACK):
+            nc.vector.tensor_tensor(part[:, t, :], dwin[t][:].indirect(lists["n4"][:]), hwin[t][:], ALU.mult)
+        res = new("res", [P, PACK, S], F32)
+        ow = new("ow", [P, S], I32)
+        osc = new("osc", [P, S], U8)
+        out_rows = out_0.rearrange("(p t) j -> p t j", t=PACK)
+        out_words = words_of(out_1)
+        for lo, hi in O_CHUNKS:
+            for t in range(PACK):
+                nc.vector.tensor_tensor(
+                    res[:, t, lo:hi], hwin[t][:].indirect(lists["n3"][:, lo // 16 : hi // 16]), part[:, t, lo:hi], ALU.mult
+                )
+            nc.sync.dma_start(out_rows[:, :, lo:hi], res[:, :, lo:hi])
+            ob = new("ob%d" % lo, [P, hi - lo, PACK], BF16)
+            dst = ob[:].rearrange("p (c i) t -> p c t i", i=4)
+            src = res[:, :, lo:hi].rearrange("p t (c i) -> p c t i", i=4)
+            if hi == S:
+                nc.vector.tensor_copy(dst, src)
+            else:
+                nc.scalar.copy(dst, src)
+            nc.vector.quantize_mx(out=ow[:, lo:hi].bitcast(FP8X4), scales=osc[:, lo:hi], in_=ob[:].rearrange("p j t -> p (j t)"))
+            nc.scalar.dma_start(out_words[:, lo:hi], ow[:, lo:hi])
+        for q in range(4):
+            eng = nc.sync if q % 2 == 0 else nc.scalar
+            eng.dma_start(out_2[0, 4 * q : 4 * q + 4, :].bitcast(I32), osc[32 * q : 32 * q + 4, :].bitcast(I32))

@@ -34,8 +34,8 @@ def tile_picked_twqpullbcube_none_po_kernel(
         keep = ctx.enter_context(tc.tile_pool(name="keep", bufs=1))
         psum = ctx.enter_context(tc.psum_pool(name="psum", bufs=1))
 
-        def new(name, shape, dtype):
-            return keep.tile(shape, dtype, name=name, align_bytes=64)
+        def new(name, shape, dtype, tag=None):
+            return keep.tile(shape, dtype, name=name, tag=tag or name, align_bytes=64)
 
         lists = {}
 
@@ -48,43 +48,41 @@ def tile_picked_twqpullbcube_none_po_kernel(
         ds = new("ds", [P, G], U8)
         dsm = new("dsm", [P, H], U8)
         xw = new("xw", [P, T], I32)
-        w1w = new("w1w", [P, H], I32)
         w2w = new("w2w", [P, H], I32)
-        dw = new("dw", [P, G], I32)
-        gain = new("gain", [P, PACK], F32)
         warm = new("warm", [P, 8], F32)
-
-        nc.vector.memset(xs[:].bitcast(I32), 0)
-        nc.gpsimd.memset(ws[:].bitcast(I32), 0)
-        nc.gpsimd.memset(warm[:], 0.0)
-        nc.scalar.activation(warm[:, 0:1], warm[:, 1:2], ACT.Sigmoid)
-        nc.vector.memset(ds[:].bitcast(I32), 0)
-        nc.vector.memset(dsm[:].bitcast(I32), 0)
         dwin = [new("dwin%d" % t, [P, 2 * S], F32) for t in range(PACK)]
         dlast = new("dlast", [P, S], F32)
         dcopy = [dwin[t + 1][:, S : 2 * S] for t in range(PACK - 1)] + [dlast[:]]
+
+        nc.gpsimd.memset(ws[:].bitcast(I32), 0)
+        nc.gpsimd.memset(warm[:], 0.0)
+        nc.scalar.activation(warm[:, 0:1], warm[:, 1:2], ACT.Sigmoid)
+        for plane in (xs, ds, dsm):
+            nc.vector.memset(plane[:].bitcast(I32), 0)
         nc.vector.memset(dwin[0][:, S : 2 * S], 0.0)
 
-        load_list("two", two)
+        def load_scales(plane, scales, k=0, queues=(nc.sync,) * 4):
+            for q in range(4):
+                queues[q].dma_start(plane[32 * q + k : 32 * q + k + 4, :].bitcast(I32), scales[0, 4 * q : 4 * q + 4, :].bitcast(I32))
+
         nc.sync.dma_start(xw[:], words_of(x_words))
+        load_list("two", two)
         load_list("offs", offs)
-        nc.sync.dma_start(w2w[:], words_of(w2_words))
-        for q in range(4):
-            nc.sync.dma_start(xs[32 * q : 32 * q + 4, :].bitcast(I32), x_scales[0, 4 * q : 4 * q + 4, :].bitcast(I32))
-        for q in range(4):
-            nc.sync.dma_start(ws[32 * q : 32 * q + 4, :].bitcast(I32), w2_scales[0, 4 * q : 4 * q + 4, :].bitcast(I32))
-        for q in range(4):
-            nc.sync.dma_start(ws[32 * q + 4 : 32 * q + 8, :].bitcast(I32), w1_scales[0, 4 * q : 4 * q + 4, :].bitcast(I32))
-        nc.sync.dma_start(w1w[:], words_of(w1_words))
         load_list("n2", n2)
         load_list("k1", k1)
-        nc.sync.dma_start(dw[:], words_of(d_words))
+        load_list("n1", n1)
+        nc.sync.dma_start(w2w[:], words_of(w2_words))
+        w1w = new("w1w", [P, H], I32)
+        nc.sync.dma_start(w1w[:], words_of(w1_words))
+        load_list("n4", n4)
+        load_list("n3", n3)
+        load_scales(xs, x_scales)
+        load_scales(ws, w2_scales)
+        load_scales(ws, w1_scales, 4)
+        gain = new("gain", [P, PACK], F32, "warm")
         nc.sync.dma_start(gain[:], gs.rearrange("(p t) o -> p (t o)", t=PACK))
         for e in range(2):
             nc.sync.dma_start(ds[e:P:16, :].bitcast(I32), d_scales[0, e:16:2, :].bitcast(I32))
-        load_list("n1", n1)
-        load_list("n4", n4)
-        load_list("n3", n3)
 
         def deal(name, src, dtype):
             dealt = new(name, [P, H], dtype)
@@ -95,8 +93,8 @@ def tile_picked_twqpullbcube_none_po_kernel(
             )
             return dealt
 
-        def pick(name, table, dtype, offsets):
-            picked = new(name, [P, S], dtype)
+        def pick(name, table, dtype, offsets, tag=None):
+            picked = new(name, [P, S], dtype, tag)
             view = U32 if dtype == I32 else U8
             nc.vector.tensor_copy(picked[:].bitcast(view), table[:].bitcast(view).indirect(offsets[:]))
             return picked
@@ -120,18 +118,19 @@ def tile_picked_twqpullbcube_none_po_kernel(
         w2d = deal("w2d", w2w, I32)
         wsd = deal("wsd", ws, U8)
         for t in range(PACK):
-            product(banks_a[t], w2d, wsd[0:P], t, xw2, xs2, 0, S)
+            product(banks_a[t], w2d, wsd, t, xw2, xs2, 0, S)
             nc.scalar.copy(dwin[t][:, 0:S], banks_a[t][:])
             nc.scalar.copy(dcopy[t], banks_a[t][:])
         xw1 = pick("xw1", xw, I32, lists["offs"])
-        xs1 = pick("xs1", xs, U8, lists["offs"])
+        xs1 = pick("xs1", xs, U8, lists["offs"], "ws")
         w1d = deal("w1d", w1w, I32)
+        dw = new("dw", [P, G], I32, "xw")
+        nc.sync.dma_start(dw[:], words_of(d_words))
         ywin = [new("ywin%d" % t, [P, 2 * S], F32) for t in range(PACK)]
+        gate = new("gate", [P, PACK, S], F32)
         for t in range(PACK):
             product(banks_b[t], w1d, wsd[4:P], t, xw1, xs1, 0, S)
             nc.scalar.activation(ywin[t][:, 0:S], banks_b[t][:], ACT.Copy, scale=gain[:, t : t + 1])
-        gate = new("gate", [P, PACK, S], F32)
-        for t in range(PACK):
             nc.vector.tensor_tensor(ywin[t][:, S : 2 * S], dwin[t][:].indirect(lists["n2"][:]), dcopy[t], ALU.subtract)
             nc.scalar.activation(gate[:, t, :], ywin[t][:, S : 2 * S], ACT.Sigmoid)
         dsg = pick("dsg", ds, U8, lists["k1"])
@@ -142,54 +141,111 @@ def tile_picked_twqpullbcube_none_po_kernel(
         dwd = deal("dwd", dwg, I32)
 
         rest = new("rest", [P, PACK, S], F32)
-        for t in range(PACK):
-            nc.vector.scalar_tensor_tensor(rest[:, t, :], gate[:, t, :], 1.0, ywin[t][:, 0:S], ALU.subtract, ALU.mult)
         pulled = new("pulled", [P, PACK, S], F32)
         zw = new("zw", [P, S], I32)
         zs = new("zs", [P, S], U8)
         banks_h = [psum.tile([P, S], F32, name="bank_h%d" % t, tag="bank_a%d" % t) for t in range(PACK)]
         hwin = [new("hwin%d" % t, [P, S], F32) for t in range(PACK)]
-        for lo, hi in Z_CHUNKS:
-            for t in range(PACK):
-                nc.vector.tensor_tensor(
-                    pulled[:, t, lo:hi], ywin[t][:].indirect(lists["n1"][:, lo // 16 : hi // 16]), gate[:, t, lo:hi], ALU.mult
-                )
-            zb = new("zb%d" % lo, [P, hi - lo, PACK], BF16)
+        zb = new("zb", [P, S, PACK], BF16)
+
+        def pull(t, lo, hi):
             nc.vector.tensor_tensor(
-                zb[:].rearrange("p (c i) t -> p c t i", i=4),
+                pulled[:, t, lo:hi], ywin[t][:].indirect(lists["n1"][:, lo // 16 : hi // 16]), gate[:, t, lo:hi], ALU.mult
+            )
+
+        def mix(lo, hi):
+            nc.vector.tensor_tensor(
+                zb[:, lo:hi, :].rearrange("p (c i) t -> p c t i", i=4),
                 pulled[:, :, lo:hi].rearrange("p t (c i) -> p c t i", i=4),
                 rest[:, :, lo:hi].rearrange("p t (c i) -> p c t i", i=4),
                 ALU.subtract,
             )
-            nc.vector.quantize_mx(out=zw[:, lo:hi].bitcast(FP8X4), scales=zs[:, lo:hi], in_=zb[:].rearrange("p j t -> p (j t)"))
-            for t in range(PACK):
-                product(banks_h[t], dwd, dsm[0:P], t, zw, zs, lo, hi)
-                nc.scalar.activation(dwin[t][:, lo:hi], banks_h[t][:, lo:hi], ACT.Tanh, scale=0.0625)
-                nc.scalar.activation(hwin[t][:, lo:hi], banks_h[t][:, lo:hi], ACT.Copy, scale=0.0625)
+
+        def quantise(words, scales, values, lo, hi):
+            nc.vector.quantize_mx(
+                out=words[:, lo:hi].bitcast(FP8X4), scales=scales[:, lo:hi], in_=values[:, lo:hi, :].rearrange("p j t -> p (j t)")
+            )
+
+        def coded(t, lo, hi):
+            product(banks_h[t], dwd, dsm, t, zw, zs, lo, hi)
+            nc.scalar.activation(dwin[t][:, lo:hi], banks_h[t][:, lo:hi], ACT.Tanh, scale=0.0625)
+            nc.scalar.activation(hwin[t][:, lo:hi], banks_h[t][:, lo:hi], ACT.Copy, scale=0.0625)
+
+        def stay(t, lo, hi):
+            nc.vector.scalar_tensor_tensor(rest[:, t, lo:hi], gate[:, t, lo:hi], 1.0, ywin[t][:, lo:hi], ALU.subtract, ALU.mult)
+
+        for t in range(PACK - 1):
+            stay(t, 0, S)
+            pull(t, 0, S)
+        stay(3, 0, 256)
+        pull(3, 0, 256)
+        stay(3, 256, S)
+        mix(0, 256)
+        pull(3, 256, S)
+        quantise(zw, zs, zb, 0, 256)
+        coded(0, 0, 256)
+        coded(1, 0, 256)
+        mix(256, 384)
+        mix(384, S)
+        quantise(zw, zs, zb, 256, 384)
+        quantise(zw, zs, zb, 384, S)
+        coded(0, 256, S)
+        coded(1, 256, S)
+        coded(2, 0, S)
+        coded(3, 0, S)
 
         part = new("part", [P, PACK, S], F32)
-        for t in range(PACK):
-            nc.vector.tensor_tensor(part[:, t, :], dwin[t][:].indirect(lists["n4"][:]), hwin[t][:], ALU.mult)
-        res = new("res", [P, PACK, S], F32)
+        res_lo = new("res_lo", [P, PACK, 256], F32)
+        res_hi = new("res_hi", [P, PACK, 256], F32, "dwin3")
+
+        def res(lo, hi):
+            return res_lo[:, :, lo:hi] if hi <= 256 else res_hi[:, :, lo - 256 : hi - 256]
+
+        ob = new("ob", [P, S, PACK], BF16)
         ow = new("ow", [P, S], I32)
         osc = new("osc", [P, S], U8)
         out_rows = out_0.rearrange("(p t) j -> p t j", t=PACK)
         out_words = words_of(out_1)
-        for lo, hi in O_CHUNKS:
-            for t in range(PACK):
-                nc.vector.tensor_tensor(
-                    res[:, t, lo:hi], hwin[t][:].indirect(lists["n3"][:, lo // 16 : hi // 16]), part[:, t, lo:hi], ALU.mult
-                )
-            nc.sync.dma_start(out_rows[:, :, lo:hi], res[:, :, lo:hi])
-            ob = new("ob%d" % lo, [P, hi - lo, PACK], BF16)
-            dst = ob[:].rearrange("p (c i) t -> p c t i", i=4)
-            src = res[:, :, lo:hi].rearrange("p t (c i) -> p c t i", i=4)
-            if hi == S:
-                nc.vector.tensor_copy(dst, src)
-            else:
-                nc.scalar.copy(dst, src)
-            nc.vector.quantize_mx(out=ow[:, lo:hi].bitcast(FP8X4), scales=osc[:, lo:hi], in_=ob[:].rearrange("p j t -> p (j t)"))
+
+        def first(t, lo, hi):
+            nc.vector.tensor_tensor(
+                part[:, t, lo:hi], dwin[t][:].indirect(lists["n4"][:, lo // 16 : hi // 16]), hwin[t][:, lo:hi], ALU.mult
+            )
+
+        def second(t, lo, hi):
+            nc.vector.tensor_tensor(
+                res(lo, hi)[:, t, :], hwin[t][:].indirect(lists["n3"][:, lo // 16 : hi // 16]), part[:, t, lo:hi], ALU.mult
+            )
+
+        def weave(copy, lo, hi):
+            nc.sync.dma_start(out_rows[:, :, lo:hi], res(lo, hi))
+            copy(
+                ob[:, lo:hi, :].rearrange("p (c i) t -> p c t i", i=4),
+                res(lo, hi).rearrange("p t (c i) -> p c t i", i=4),
+            )
+
+        def hand_on(lo, hi):
+            quantise(ow, osc, ob, lo, hi)
             nc.scalar.dma_start(out_words[:, lo:hi], ow[:, lo:hi])
+
+        first(0, 0, 256)
+        first(0, 256, 512)
+        for t in range(1, PACK):
+            first(t, 0, S)
+            second(t - 1, 0, 256)
+        second(0, 256, 384)
+        second(3, 0, 256)
+        weave(nc.scalar.copy, 0, 256)
+        for t in range(1, PACK):
+            second(t, 256, 384)
+        weave(nc.scalar.copy, 256, 384)
+        for t in range(PACK - 1):
+            second(t, 384, 512)
+        hand_on(0, 256)
+        second(3, 384, 512)
+        hand_on(256, 384)
+        weave(nc.vector.tensor_copy, 384, 512)
+        hand_on(384, 512)
         for q in range(4):
             eng = nc.sync if q % 2 == 0 else nc.scalar
             eng.dma_start(out_2[0, 4 * q : 4 * q + 4, :].bitcast(I32), osc[32 * q : 32 * q + 4, :].bitcast(I32))

@@ -44,7 +44,8 @@ def tile_picked_twqpullbcube_none_po_kernel(
             nc.sync.dma_start(lists[name][:], ap)
 
         xs = new("xs", [P, T], U8)
-        ws = new("ws", [P, H], U8)
+        w2s = new("w2s", [P, H], U8)
+        w1s = new("w1s", [P, H], U8)
         ds = new("ds", [P, G], U8)
         dsm = new("dsm", [P, H], U8)
         xw = new("xw", [P, T], I32)
@@ -54,10 +55,9 @@ def tile_picked_twqpullbcube_none_po_kernel(
         dlast = new("dlast", [P, S], F32)
         dcopy = [dwin[t + 1][:, S : 2 * S] for t in range(PACK - 1)] + [dlast[:]]
 
-        nc.gpsimd.memset(ws[:].bitcast(I32), 0)
         nc.gpsimd.memset(warm[:], 0.0)
         nc.scalar.activation(warm[:, 0:1], warm[:, 1:2], ACT.Sigmoid)
-        for plane in (xs, ds, dsm):
+        for plane in (xs, w2s, w1s, ds, dsm):
             nc.vector.memset(plane[:].bitcast(I32), 0)
         nc.vector.memset(dwin[0][:, S : 2 * S], 0.0)
 
@@ -65,20 +65,18 @@ def tile_picked_twqpullbcube_none_po_kernel(
             for q in range(4):
                 queues[q].dma_start(plane[32 * q + k : 32 * q + k + 4, :].bitcast(I32), scales[0, 4 * q : 4 * q + 4, :].bitcast(I32))
 
-        nc.sync.dma_start(xw[:], words_of(x_words))
         load_list("two", two)
+        nc.sync.dma_start(xw[:], words_of(x_words))
         load_list("offs", offs)
         load_list("n2", n2)
         load_list("k1", k1)
         load_list("n1", n1)
-        nc.sync.dma_start(w2w[:], words_of(w2_words))
-        w1w = new("w1w", [P, H], I32)
-        nc.sync.dma_start(w1w[:], words_of(w1_words))
         load_list("n4", n4)
+        nc.sync.dma_start(w2w[:], words_of(w2_words))
         load_list("n3", n3)
         load_scales(xs, x_scales)
-        load_scales(ws, w2_scales)
-        load_scales(ws, w1_scales, 4)
+        load_scales(w2s, w2_scales)
+        load_scales(w1s, w1_scales)
         gain = new("gain", [P, PACK], F32, "warm")
         nc.sync.dma_start(gain[:], gs.rearrange("(p t) o -> p (t o)", t=PACK))
         for e in range(2):
@@ -90,6 +88,15 @@ def tile_picked_twqpullbcube_none_po_kernel(
             nc.vector.tensor_copy(
                 dealt[:].bitcast(view).rearrange("p (t m) -> p m t", t=PACK),
                 src[:].bitcast(view).rearrange("p (m t) -> p m t", t=PACK),
+            )
+            return dealt
+
+        def deal_aside(name, src, dtype):
+            dealt = new(name, [P, H], dtype)
+            view = U32 if dtype == I32 else U8
+            nc.gpsimd.tensor_copy(
+                dealt[:].bitcast(view).rearrange("p (t m) -> p t m", t=PACK),
+                src[:].bitcast(view).rearrange("p (m t) -> p t m", t=PACK),
             )
             return dealt
 
@@ -115,21 +122,24 @@ def tile_picked_twqpullbcube_none_po_kernel(
 
         xw2 = pick("xw2", xw, I32, lists["two"])
         xs2 = pick("xs2", xs, U8, lists["two"])
-        w2d = deal("w2d", w2w, I32)
-        wsd = deal("wsd", ws, U8)
+        w2d = deal_aside("w2d", w2w, I32)
+        w2sd = deal_aside("w2sd", w2s, U8)
+        w1w = new("w1w", [P, H], I32, "w2w")
+        nc.sync.dma_start(w1w[:], words_of(w1_words))
         for t in range(PACK):
-            product(banks_a[t], w2d, wsd, t, xw2, xs2, 0, S)
+            product(banks_a[t], w2d, w2sd, t, xw2, xs2, 0, S)
             nc.scalar.copy(dwin[t][:, 0:S], banks_a[t][:])
             nc.scalar.copy(dcopy[t], banks_a[t][:])
         xw1 = pick("xw1", xw, I32, lists["offs"])
-        xs1 = pick("xs1", xs, U8, lists["offs"], "ws")
-        w1d = deal("w1d", w1w, I32)
+        xs1 = pick("xs1", xs, U8, lists["offs"])
+        w1d = deal_aside("w1d", w1w, I32)
+        w1sd = deal_aside("w1sd", w1s, U8)
         dw = new("dw", [P, G], I32, "xw")
         nc.sync.dma_start(dw[:], words_of(d_words))
         ywin = [new("ywin%d" % t, [P, 2 * S], F32) for t in range(PACK)]
         gate = new("gate", [P, PACK, S], F32)
         for t in range(PACK):
-            product(banks_b[t], w1d, wsd[4:P], t, xw1, xs1, 0, S)
+            product(banks_b[t], w1d, w1sd, t, xw1, xs1, 0, S)
             nc.scalar.activation(ywin[t][:, 0:S], banks_b[t][:], ACT.Copy, scale=gain[:, t : t + 1])
             nc.vector.tensor_tensor(ywin[t][:, S : 2 * S], dwin[t][:].indirect(lists["n2"][:]), dcopy[t], ALU.subtract)
             nc.scalar.activation(gate[:, t, :], ywin[t][:, S : 2 * S], ACT.Sigmoid)
@@ -171,6 +181,8 @@ def tile_picked_twqpullbcube_none_po_kernel(
             nc.scalar.activation(dwin[t][:, lo:hi], banks_h[t][:, lo:hi], ACT.Tanh, scale=0.0625)
             nc.scalar.activation(hwin[t][:, lo:hi], banks_h[t][:, lo:hi], ACT.Copy, scale=0.0625)
 
+        bank_end = psum.tile([P, S], F32, name="bank_end", tag="bank_b0")
+
         def stay(t, lo, hi):
             nc.vector.scalar_tensor_tensor(rest[:, t, lo:hi], gate[:, t, lo:hi], 1.0, ywin[t][:, lo:hi], ALU.subtract, ALU.mult)
 
@@ -189,7 +201,12 @@ def tile_picked_twqpullbcube_none_po_kernel(
         mix(384, S)
         quantise(zw, zs, zb, 256, 384)
         quantise(zw, zs, zb, 384, S)
-        coded(0, 256, S)
+        product(banks_h[0], dwd, dsm, 0, zw, zs, 256, 384)
+        product(bank_end, dwd, dsm, 0, zw, zs, 384, S)
+        nc.scalar.activation(dwin[0][:, 256:384], banks_h[0][:, 256:384], ACT.Tanh, scale=0.0625)
+        nc.scalar.activation(dwin[0][:, 384:S], bank_end[:, 384:S], ACT.Tanh, scale=0.0625)
+        nc.scalar.activation(hwin[0][:, 256:384], banks_h[0][:, 256:384], ACT.Copy, scale=0.0625)
+        nc.scalar.activation(hwin[0][:, 384:S], bank_end[:, 384:S], ACT.Copy, scale=0.0625)
         coded(1, 256, S)
         coded(2, 0, S)
         coded(3, 0, S)
@@ -217,35 +234,43 @@ def tile_picked_twqpullbcube_none_po_kernel(
                 res(lo, hi)[:, t, :], hwin[t][:].indirect(lists["n3"][:, lo // 16 : hi // 16]), part[:, t, lo:hi], ALU.mult
             )
 
+        def store(t0, t1, lo, hi):
+            nc.sync.dma_start(out_rows[:, t0:t1, lo:hi], res(lo, hi)[:, t0:t1, :])
+
         def weave(copy, lo, hi):
-            nc.sync.dma_start(out_rows[:, :, lo:hi], res(lo, hi))
             copy(
                 ob[:, lo:hi, :].rearrange("p (c i) t -> p c t i", i=4),
                 res(lo, hi).rearrange("p t (c i) -> p c t i", i=4),
             )
 
-        def hand_on(lo, hi):
-            quantise(ow, osc, ob, lo, hi)
-            nc.scalar.dma_start(out_words[:, lo:hi], ow[:, lo:hi])
-
         first(0, 0, 256)
-        first(0, 256, 512)
-        for t in range(1, PACK):
-            first(t, 0, S)
-            second(t - 1, 0, 256)
-        second(0, 256, 384)
+        first(0, 256, S)
+        first(1, 0, S)
+        second(0, 0, 256)
+        first(2, 0, S)
+        second(1, 0, 256)
+        store(0, 2, 0, 256)
+        first(3, 0, S)
+        second(2, 0, 256)
+        second(0, 256, S)
         second(3, 0, 256)
+        store(2, 4, 0, 256)
         weave(nc.scalar.copy, 0, 256)
-        for t in range(1, PACK):
-            second(t, 256, 384)
+        second(1, 256, S)
+        store(0, 2, 256, S)
+        second(2, 256, 384)
+        second(3, 256, 384)
+        store(2, 4, 256, 384)
         weave(nc.scalar.copy, 256, 384)
-        for t in range(PACK - 1):
-            second(t, 384, 512)
-        hand_on(0, 256)
-        second(3, 384, 512)
-        hand_on(256, 384)
-        weave(nc.vector.tensor_copy, 384, 512)
-        hand_on(384, 512)
+        second(2, 384, S)
+        second(3, 384, S)
+        store(2, 4, 384, S)
+        quantise(ow, osc, ob, 0, 256)
+        nc.scalar.dma_start(out_words[:, 0:256], ow[:, 0:256])
+        weave(nc.vector.tensor_copy, 384, S)
+        quantise(ow, osc, ob, 256, 384)
+        quantise(ow, osc, ob, 384, S)
+        nc.sync.dma_start(out_words[:, 256:S], ow[:, 256:S])
         for q in range(4):
-            eng = nc.sync if q % 2 == 0 else nc.scalar
+            eng = nc.scalar if q % 2 == 0 else nc.sync
             eng.dma_start(out_2[0, 4 * q : 4 * q + 4, :].bitcast(I32), osc[32 * q : 32 * q + 4, :].bitcast(I32))

@@ -50,13 +50,10 @@ def tile_picked_twqpullbcube_none_po_kernel(
         dsm = new("dsm", [P, H], U8)
         xw = new("xw", [P, T], I32)
         w2w = new("w2w", [P, H], I32)
-        warm = new("warm", [P, 8], F32)
         dwin = [new("dwin%d" % t, [P, 2 * S], F32) for t in range(PACK)]
         dlast = new("dlast", [P, S], F32)
         dcopy = [dwin[t + 1][:, S : 2 * S] for t in range(PACK - 1)] + [dlast[:]]
 
-        nc.gpsimd.memset(warm[:], 0.0)
-        nc.scalar.activation(warm[:, 0:1], warm[:, 1:2], ACT.Sigmoid)
         for plane in (xs, w2s, w1s, ds, dsm):
             nc.vector.memset(plane[:].bitcast(I32), 0)
         nc.vector.memset(dwin[0][:, S : 2 * S], 0.0)
@@ -77,8 +74,8 @@ def tile_picked_twqpullbcube_none_po_kernel(
         load_scales(xs, x_scales)
         load_scales(w2s, w2_scales)
         load_scales(w1s, w1_scales)
-        gain = new("gain", [P, PACK], F32, "warm")
-        nc.sync.dma_start(gain[:], gs.rearrange("(p t) o -> p (t o)", t=PACK))
+        gain = new("gain", [P, PACK], F32)
+        nc.gpsimd.dma_start(gain[:], gs.rearrange("(p t) o -> p (t o)", t=PACK))
         for e in range(2):
             nc.sync.dma_start(ds[e:P:16, :].bitcast(I32), d_scales[0, e:16:2, :].bitcast(I32))
 

from contextlib import ExitStack

import concourse.mybir as mybir

K, T, S, H, G = 512, 1024, 512, 512, 2048
FLOPS = 3 * 2 * 512 * 512 * 512

F32 = mybir.dt.float32
BF16 = mybir.dt.bfloat16
I32 = mybir.dt.int32
U32 = mybir.dt.uint32
U16 = mybir.dt.uint16
U8 = mybir.dt.uint8
FP8X4 = mybir.dt.float8_e4m3fn_x4
ALU = mybir.AluOpType
ACT = mybir.ActivationFunctionType

P = 128
PACK = 4
Z_CHUNKS = ((0, 256), (256, 384), (384, 512))
O_CHUNKS = ((0, 256), (256, 384), (384, 512))


def tile_picked_twqpullbcube_none_po_kernel(
    tc, x_words, x_scales, w1_words, w1_scales, w2_words, w2_scales, gs, d_words, d_scales,
    offs, two, n1, n2, k1, n3, n4, out_0, out_1, out_2,
):
    nc = tc.nc

    def words_of(ap):
        return ap[0].rearrange("p n t -> p (n t)").bitcast(I32)

    with ExitStack() as ctx:
        keep = ctx.enter_context(tc.tile_pool(name="keep", bufs=1))
        psum = ctx.enter_context(tc.psum_pool(name="psum", bufs=1))

        def new(name, shape, dtype, tag=None):
            return keep.tile(shape, dtype, name=name, tag=tag or name, align_bytes=64)

        lists = {}

        def load_list(name, ap):
            lists[name] = new("list_" + name, [P, S // 16], U16)
            nc.sync.dma_start(lists[name][:], ap)

        xs = new("xs", [P, T], U8)
        w2s = new("w2s", [P, H], U8)
        w1s = new("w1s", [P, H], U8)
        ds = new("ds", [P, G], U8)
        dsm = new("dsm", [P, H], U8)
        xw = new("xw", [P, T], I32)
        w2w = new("w2w", [P, H], I32)
        dwin = [new("dwin%d" % t, [P, 2 * S], F32) for t in range(PACK)]
        dlast = new("dlast", [P, S], F32)
        dcopy = [dwin[t + 1][:, S : 2 * S] for t in range(PACK - 1)] + [dlast[:]]

        for plane in (xs, w2s, w1s, ds, dsm):
            nc.vector.memset(plane[:].bitcast(I32), 0)
        nc.vector.memset(dwin[0][:, S : 2 * S], 0.0)

        def load_scales(plane, scales, k=0, queues=(nc.sync,) * 4):
            for q in range(4):
                queues[q].dma_start(plane[32 * q + k : 32 * q + k + 4, :].bitcast(I32), scales[0, 4 * q : 4 * q + 4, :].bitcast(I32))

        load_list("two", two)
        nc.sync.dma_start(xw[:], words_of(x_words))
        load_list("offs", offs)
        load_list("n2", n2)
        load_list("k1", k1)
        load_list("n1", n1)
        load_list("n4", n4)
        nc.sync.dma_start(w2w[:], words_of(w2_words))
        load_list("n3", n3)
        load_scales(xs, x_scales)
        load_scales(w2s, w2_scales)
        load_scales(w1s, w1_scales)
        gain = new("gain", [P, PACK], F32)
        nc.gpsimd.dma_start(gain[:], gs.rearrange("(p t) o -> p (t o)", t=PACK))
        for e in range(2):
            nc.sync.dma_start(ds[e:P:16, :].bitcast(I32), d_scales[0, e:16:2, :].bitcast(I32))

        def deal(name, src, dtype):
            dealt = new(name, [P, H], dtype)
            view = U32 if dtype == I32 else U8
            nc.vector.tensor_copy(
                dealt[:].bitcast(view).rearrange("p (t m) -> p m t", t=PACK),
                src[:].bitcast(view).rearrange("p (m t) -> p m t", t=PACK),
            )
            return dealt

        def deal_aside(name, src, dtype):
            dealt = new(name, [P, H], dtype)
            view = U32 if dtype == I32 else U8
            nc.gpsimd.tensor_copy(
                dealt[:].bitcast(view).rearrange("p (t m) -> p t m", t=PACK),
                src[:].bitcast(view).rearrange("p (m t) -> p t m", t=PACK),
            )
            return dealt

        def pick(name, table, dtype, offsets, tag=None):
            picked = new(name, [P, S], dtype, tag)
            view = U32 if dtype == I32 else U8
            nc.vector.tensor_copy(picked[:].bitcast(view), table[:].bitcast(view).indirect(offsets[:]))
            return picked

        banks_a = [psum.tile([P, S], F32, name="bank_a%d" % t, tag="bank_a%d" % t) for t in range(PACK)]
        banks_b = [psum.tile([P, S], F32, name="bank_b%d" % t, tag="bank_b%d" % t) for t in range(PACK)]

        def product(bank, words, scales, t, mov_words, mov_scales, lo, hi):
            nc.tensor.matmul_mx(
                out=bank[:, lo:hi],
                lhsT=words[:, P * t : P * (t + 1)].bitcast(FP8X4),
                lhsT_scale=scales[:, P * t : P * (t + 1)],
                rhs=mov_words[:, lo:hi].bitcast(FP8X4),
                rhs_scale=mov_scales[:, lo:hi],
                start=True,
                stop=True,
            )

        xw2 = pick("xw2", xw, I32, lists["two"])
        xs2 = pick("xs2", xs, U8, lists["two"])
        w2d = deal_aside("w2d", w2w, I32)
        w2sd = deal_aside("w2sd", w2s, U8)
        w1w = new("w1w", [P, H], I32, "w2w")
        nc.sync.dma_start(w1w[:], words_of(w1_words))
        for t in range(PACK):
            product(banks_a[t], w2d, w2sd, t, xw2, xs2, 0, S)
            nc.scalar.copy(dwin[t][:, 0:S], banks_a[t][:])
            nc.scalar.copy(dcopy[t], banks_a[t][:])
        xw1 = pick("xw1", xw, I32, lists["offs"])
        xs1 = pick("xs1", xs, U8, lists["offs"])
        w1d = deal_aside("w1d", w1w, I32)
        w1sd = deal_aside("w1sd", w1s, U8)
        dw = new("dw", [P, G], I32, "xw")
        nc.sync.dma_start(dw[:], words_of(d_words))
        ywin = [new("ywin%d" % t, [P, 2 * S], F32) for t in range(PACK)]
        gate = new("gate", [P, PACK, S], F32)
        for t in range(PACK):
            product(banks_b[t], w1d, w1sd, t, xw1, xs1, 0, S)
            nc.scalar.activation(ywin[t][:, 0:S], banks_b[t][:], ACT.Copy, scale=gain[:, t : t + 1])
            nc.vector.tensor_tensor(ywin[t][:, S : 2 * S], dwin[t][:].indirect(lists["n2"][:]), dcopy[t], ALU.subtract)
            nc.scalar.activation(gate[:, t, :], ywin[t][:, S : 2 * S], ACT.Sigmoid)
        dsg = pick("dsg", ds, U8, lists["k1"])
        dsd = deal("dsd", dsg, U8)
        for r, src in enumerate((0, 1, 16, 17)):
            nc.sync.dma_start(dsm[r:P:32, :].bitcast(I32), dsd[src:P:32, :].bitcast(I32))
        dwg = pick("dwg", dw, I32, lists["k1"])
        dwd = deal("dwd", dwg, I32)

        rest = new("rest", [P, PACK, S], F32)
        pulled = new("pulled", [P, PACK, S], F32)
        zw = new("zw", [P, S], I32)
        zs = new("zs", [P, S], U8)
        banks_h = [psum.tile([P, S], F32, name="bank_h%d" % t, tag="bank_a%d" % t) for t in range(PACK)]
        hwin = [new("hwin%d" % t, [P, S], F32) for t in range(PACK)]
        zb = new("zb", [P, S, PACK], BF16)

        def pull(t, lo, hi):
            nc.vector.tensor_tensor(
                pulled[:, t, lo:hi], ywin[t][:].indirect(lists["n1"][:, lo // 16 : hi // 16]), gate[:, t, lo:hi], ALU.mult
            )

        def mix(lo, hi):
            nc.vector.tensor_tensor(
                zb[:, lo:hi, :].rearrange("p (c i) t -> p c t i", i=4),
                pulled[:, :, lo:hi].rearrange("p t (c i) -> p c t i", i=4),
                rest[:, :, lo:hi].rearrange("p t (c i) -> p c t i", i=4),
                ALU.subtract,
            )

        def quantise(words, scales, values, lo, hi):
            nc.vector.quantize_mx(
                out=words[:, lo:hi].bitcast(FP8X4), scales=scales[:, lo:hi], in_=values[:, lo:hi, :].rearrange("p j t -> p (j t)")
            )

        def coded(t, lo, hi):
            product(banks_h[t], dwd, dsm, t, zw, zs, lo, hi)
            nc.scalar.activation(dwin[t][:, lo:hi], banks_h[t][:, lo:hi], ACT.Tanh, scale=0.0625)
            nc.scalar.activation(hwin[t][:, lo:hi], banks_h[t][:, lo:hi], ACT.Copy, scale=0.0625)

        bank_end = psum.tile([P, S], F32, name="bank_end", tag="bank_b0")

        def stay(t, lo, hi):
            nc.vector.scalar_tensor_tensor(rest[:, t, lo:hi], gate[:, t, lo:hi], 1.0, ywin[t][:, lo:hi], ALU.subtract, ALU.mult)

        for t in range(PACK - 1):
            stay(t, 0, S)
            pull(t, 0, S)
        stay(3, 0, 256)
        pull(3, 0, 256)
        stay(3, 256, S)
        mix(0, 256)
        pull(3, 256, S)
        quantise(zw, zs, zb, 0, 256)
        coded(0, 0, 256)
        coded(1, 0, 256)
        mix(256, 384)
        mix(384, S)
        quantise(zw, zs, zb, 256, 384)
        quantise(zw, zs, zb, 384, S)
        product(banks_h[0], dwd, dsm, 0, zw, zs, 256, 384)
        product(bank_end, dwd, dsm, 0, zw, zs, 384, S)
        nc.scalar.activation(dwin[0][:, 256:384], banks_h[0][:, 256:384], ACT.Tanh, scale=0.0625)
        nc.scalar.activation(dwin[0][:, 384:S], bank_end[:, 384:S], ACT.Tanh, scale=0.0625)
        nc.scalar.activation(hwin[0][:, 256:384], banks_h[0][:, 256:384], ACT.Copy, scale=0.0625)
        nc.scalar.activation(hwin[0][:, 384:S], bank_end[:, 384:S], ACT.Copy, scale=0.0625)
        coded(1, 256, S)
        coded(2, 0, S)
        coded(3, 0, S)

        part = new("part", [P, PACK, S], F32)
        res_lo = new("res_lo", [P, PACK, 256], F32)
        res_hi = new("res_hi", [P, PACK, 256], F32, "dwin3")

        def res(lo, hi):
            return res_lo[:, :, lo:hi] if hi <= 256 else res_hi[:, :, lo - 256 : hi - 256]

        ob = new("ob", [P, S, PACK], BF16)
        ow = new("ow", [P, S], I32)
        osc = new("osc", [P, S], U8)
        out_rows = out_0.rearrange("(p t) j -> p t j", t=PACK)
        out_words = words_of(out_1)

        def first(t, lo, hi):
            nc.vector.tensor_tensor(
                part[:, t, lo:hi], dwin[t][:].indirect(lists["n4"][:, lo // 16 : hi // 16]), hwin[t][:, lo:hi], ALU.mult
            )

        def second(t, lo, hi):
            nc.vector.tensor_tensor(
                res(lo, hi)[:, t, :], hwin[t][:].indirect(lists["n3"][:, lo // 16 : hi // 16]), part[:, t, lo:hi], ALU.mult
            )

        def store(t0, t1, lo, hi):
            nc.sync.dma_start(out_rows[:, t0:t1, lo:hi], res(lo, hi)[:, t0:t1, :])

        def weave(copy, lo, hi):
            copy(
                ob[:, lo:hi, :].rearrange("p (c i) t -> p c t i", i=4),
                res(lo, hi).rearrange("p t (c i) -> p c t i", i=4),
            )

        first(0, 0, 256)
        first(0, 256, S)
        first(1, 0, S)
        second(0, 0, 256)
        first(2, 0, S)
        second(1, 0, 256)
        store(0, 2, 0, 256)
        first(3, 0, S)
        second(2, 0, 256)
        second(0, 256, S)
        second(3, 0, 256)
        store(2, 4, 0, 256)
        weave(nc.scalar.copy, 0, 256)
        second(1, 256, S)
        store(0, 2, 256, S)
        second(2, 256, 384)
        second(3, 256, 384)
        store(2, 4, 256, 384)
        weave(nc.scalar.copy, 256, 384)
        second(2, 384, S)
        second(3, 384, S)
        store(2, 4, 384, S)
        quantise(ow, osc, ob, 0, 256)
        nc.scalar.dma_start(out_words[:, 0:256], ow[:, 0:256])
        weave(nc.vector.tensor_copy, 384, S)
        quantise(ow, osc, ob, 256, 384)
        quantise(ow, osc, ob, 384, S)
        nc.sync.dma_start(out_words[:, 256:S], ow[:, 256:S])
        for q in range(4):
            eng = nc.scalar if q % 2 == 0 else nc.sync
            eng.dma_start(out_2[0, 4 * q : 4 * q + 4, :].bitcast(I32), osc[32 * q : 32 * q + 4, :].bitcast(I32))
